import numpy as np
import ml_dtypes


def mxq(x, axis, fmt="e4m3"):
    dtype, down = {"e4m3": (ml_dtypes.float8_e4m3fn, 7), "e5m2": (ml_dtypes.float8_e5m2, 14)}[fmt]
    v = np.moveaxis(np.asarray(x, np.float32).astype(ml_dtypes.bfloat16).astype(np.float64), axis, -1)
    blocks = v.reshape(v.shape[:-1] + (-1, 32))
    amax = np.abs(blocks).max(-1, keepdims=True)
    byte = np.maximum(np.where(amax > 0, np.frexp(amax)[1] - 1 + 127, 0) - down, 1)
    scale = np.exp2(byte - 127.0)
    codes = (blocks / scale).astype(np.float32).astype(dtype).astype(np.float64)
    return np.moveaxis((codes * scale).reshape(v.shape), -1, axis)


WIDE = False


def mx_kscale(k):
    if not WIDE:
        return np.ones(k)
    levels = np.array([10, -10, 5, -5, 0])
    if k % 512:
        return np.exp2(np.random.permutation(np.resize(levels, k // 32))).repeat(32)
    a = np.empty((k // 512, 16))
    for p in range(k // 512):
        a[p, :8] = np.random.permutation(np.resize(levels, 8))
        for g in range(8):
            far = levels[np.abs(levels - a[p, g]) >= 10]
            a[p, g + 8] = far[np.random.randint(len(far))]
    return np.exp2(a.ravel()).repeat(32)


def f64(x):
    return np.asarray(x).astype(np.float64)


def striped(idx):
    return np.tile(idx.reshape(-1, 16).T, (8, 1)).astype(np.uint16)


def unstriped(offs):
    return offs[:16].T.reshape(-1).astype(np.int64)


def pack_weight(w):
    k, n = w.shape
    w = f64(np.asarray(w, np.float32).astype(ml_dtypes.bfloat16)).reshape(k // 32, 32, n)
    amax = np.abs(w).max(1)
    byte = np.clip(np.where(amax > 0, np.frexp(amax)[1] - 1 + 127 - 7, 1), 1, 254)
    scaled = (w * np.exp2(127.0 - byte)[:, None, :]).reshape(k, n).astype(np.float32)
    words = np.ascontiguousarray(scaled.reshape(k // 512, 128, 4, n).transpose(0, 1, 3, 2)).astype(ml_dtypes.float8_e4m3fn).view(np.uint8)
    return words, np.ascontiguousarray(byte.astype(np.uint8).reshape(k // 512, 16, n))


def unpack_weight(words, scales):
    g, p, n, _ = words.shape
    vals = np.ascontiguousarray(words).view(ml_dtypes.float8_e4m3fn).astype(np.float64) * np.repeat(np.exp2(scales.astype(np.float64) - 127.0), 8, axis=1)[..., None]
    return vals.transpose(0, 1, 3, 2).reshape(g * 512, n)


def sigmoid(v):
    return 1.0 / (1.0 + np.exp(-np.maximum(v, -700.0)))


K, T, S, D, N, H, V, U = 512, 2048, 1024, 4, 128, 512, 256, 512


def setup_inputs():
    n = np.random.standard_normal
    s = mx_kscale(K)[:, None]
    u = mx_kscale(H)
    packed_xT = pack_weight(n((K, T)) * s)
    return {
        "x_words": packed_xT[0],
        "x_scales": packed_xT[1],
        "w1": (n((K, H)) / np.sqrt(K) / s).astype(np.float32),
        "w2": (n((K, H)) / np.sqrt(K) / s).astype(np.float32),
        "ref": (np.random.uniform(0.5, 2.5, (H, S))).astype(np.float32),
        "wt": (np.random.uniform(0.4, 1.6, (H, U))).astype(np.float32),
        "unit": (np.random.uniform(0.6, 1.4, (H, 1)) * u[:, None]).astype(np.float32),
        "w3": (n((H, N)) / np.sqrt(H) / u[:, None]).astype(np.float32),
        "offs": striped(np.random.permutation(T)[:S]),
        "par": striped(np.random.permutation(S)),
        "dom": striped(np.random.permutation(np.concatenate([np.arange(V), np.random.randint(0, V, U - V)]))),
    }


def reference(x_words, x_scales, w1, w2, ref, wt, unit, w3, offs, par, dom):
    xq = unpack_weight(x_words, x_scales)[:, unstriped(offs)]
    px = mxq(f64(w1), 0, "e4m3").T @ xq
    xp = px[:, unstriped(par)]
    py = mxq(f64(w2), 0, "e4m3").T @ xq
    yp = py[:, unstriped(par)]
    dis = np.sqrt((px - xp) ** 2 + (py - yp) ** 2 + 0.05)
    err = np.abs(dis - f64(ref))
    s1 = sigmoid(-4.0 * err + 2.0)
    s2 = sigmoid(-4.0 * err + 5.0)
    sc = 0.5 * (s1 + s2)
    lddt = sc.reshape(len(sc), -1, D).mean(axis=2)
    md = lddt[:, unstriped(dom)]
    hid = f64(unit) * (md * f64(wt))
    return mxq(f64(w3), 0, "e4m3").T @ mxq(hid, 0, "e4m3")

@@ -1,0 +1,309 @@
+from contextlib import ExitStack
+
+import concourse.mybir as mybir
+from concourse.masks import make_identity
+
+F32 = mybir.dt.float32
+BF16 = mybir.dt.bfloat16
+I32 = mybir.dt.int32
+U32 = mybir.dt.uint32
+U16 = mybir.dt.uint16
+U8 = mybir.dt.uint8
+FP8X4 = mybir.dt.float8_e4m3fn_x4
+ALU = mybir.AluOpType
+ACT = mybir.ActivationFunctionType
+
+P = 128
+K, T, S, D, N, H, V, U = 512, 2048, 1024, 4, 128, 512, 256, 512
+PACK = 4
+HALF = 512
+LIST = 16
+LDDT_ON_SCALAR = (0,)
+
+FLOPS = 2 * 2 * K * H * S + 2 * H * N * U
+
+
+def tile_picked_ylddts_mean_p_kernel(
+    tc, x_words, x_scales, w1, w2, ref, wt, unit, w3, offs, par, dom, out
+):
+    nc = tc.nc
+    with ExitStack() as ctx:
+        keep = ctx.enter_context(tc.tile_pool(name="keep", bufs=1))
+        ring = ctx.enter_context(tc.tile_pool(name="ring", bufs=4))
+        psum = ctx.enter_context(tc.psum_pool(name="psum", bufs=1))
+
+        offs_sb = keep.tile([P, S // LIST], U16, name="offs_sb")
+        par_sb = keep.tile([P, S // LIST], U16, name="par_sb")
+        dom_sb = keep.tile([P, U // LIST], U16, name="dom_sb")
+        x_bytes = keep.tile([P, T], U8, name="x_bytes", align_bytes=64)
+        x_codes = keep.tile([P, T], U32, name="x_codes", align_bytes=64)
+        w1_raw = ring.tile([P, PACK, H], F32, name="big", bufs=2)
+        w2_raw = ring.tile([P, PACK, H], F32, name="big", bufs=2)
+        unit_sb = keep.tile([P, PACK], F32, name="unit_sb")
+        ident = keep.tile([P, P], F32, name="ident")
+
+        nc.gpsimd.memset(x_bytes[:].bitcast(I32), 0)
+        nc.sync.dma_start(offs_sb[:], offs)
+        nc.sync.dma_start(par_sb[:], par)
+        nc.sync.dma_start(dom_sb[:], dom)
+        for q in range(4):
+            nc.sync.dma_start(
+                x_bytes[32 * q : 32 * q + 4, :].bitcast(I32),
+                x_scales[0, 4 * q : 4 * q + 4, :].bitcast(I32),
+            )
+        nc.sync.dma_start(
+            x_codes[:].bitcast(I32), x_words[0].rearrange("p n t -> p (n t)").bitcast(I32)
+        )
+        nc.sync.dma_start(w1_raw[:], w1.rearrange("(p j) c -> p j c", j=PACK))
+        nc.sync.dma_start(w2_raw[:], w2.rearrange("(p j) c -> p j c", j=PACK))
+        make_identity(nc, ident[:])
+
+        ref_rows = ref.rearrange("(p t) j -> p t j", t=PACK)
+        wt_rows = wt.rearrange("(p t) r -> p t r", t=PACK)
+        ref_sb = {}
+
+        def load_ref(pair):
+            both = ring.tile([P, 2, S], F32, name="big", bufs=2)
+            nc.sync.dma_start(both[:], ref_rows[:, 2 * pair : 2 * pair + 2, :])
+            for n in range(2):
+                ref_sb[2 * pair + n] = both[:, n, :]
+
+        nc.sync.dma_start(unit_sb[:], unit.rearrange("(p t) o -> p (t o)", t=PACK))
+
+        eighth = keep.tile([P, PACK], F32, name="eighth")
+        nc.gpsimd.tensor_scalar(eighth[:], unit_sb[:], 0.125, 0.0, ALU.mult, ALU.add)
+
+        picked_bytes = keep.tile([P, S], U8, name="picked_bytes", align_bytes=64)
+        nc.vector.tensor_copy(picked_bytes[:], x_bytes[:].indirect(offs_sb[:]))
+        picked_codes = []
+        for h in range(2):
+            codes = keep.tile([P, HALF], U32, name="picked_codes%d" % h, align_bytes=64)
+            nc.vector.tensor_copy(
+                codes[:], x_codes[:].indirect(offs_sb[:, h * 32 : (h + 1) * 32])
+            )
+            picked_codes.append(codes)
+
+        weights = {}
+
+        def deal(name, raw, t0, t1, engine):
+            width = (t1 - t0) * P
+            dealt = keep.tile([P, width * PACK], BF16, name=name + "_bf", align_bytes=64)
+            dst = dealt[:].rearrange("p (t m j) -> p m j t", j=PACK, m=P)
+            src = raw[:].rearrange("p j (m t) -> p m j t", t=PACK)[:, :, :, t0:t1]
+            if engine == "vector":
+                nc.vector.tensor_copy(dst, src)
+            else:
+                nc.scalar.copy(dst, src)
+            return dealt
+
+        def quantise(name, dealt, width):
+            codes = keep.tile([P, width], U32, name=name + "_codes", align_bytes=64)
+            scales = keep.tile([P, width], U8, name=name + "_scales", align_bytes=64)
+            nc.vector.quantize_mx(out=codes[:].bitcast(FP8X4), scales=scales[:], in_=dealt[:])
+            return codes, scales
+
+        window, twin, diff, square, dist, err = {}, {}, {}, {}, {}, {}
+
+        def product(c, t):
+            codes, scales, col = weights[c, t]
+            window[c, t] = keep.tile([P, S], F32, name="window%s%d" % (c, t))
+            tag = "signed" if (c, t) == ("y", PACK - 1) else "twin%s%d" % (c, t)
+            whole = keep.tile([P, S], F32, name=tag)
+            for h in range(2):
+                twin[c, t, h] = whole[:, h * HALF : (h + 1) * HALF]
+            for h in range(2):
+                cols = slice(h * HALF, (h + 1) * HALF)
+                bank = psum.tile([P, HALF], F32, name="wide", bufs=6)
+                nc.tensor.matmul_mx(
+                    out=bank[:],
+                    lhsT=codes[:, col : col + P].bitcast(FP8X4),
+                    lhsT_scale=scales[:, col : col + P],
+                    rhs=picked_codes[h][:].bitcast(FP8X4),
+                    rhs_scale=picked_bytes[:, cols],
+                    start=True,
+                    stop=True,
+                )
+                nc.scalar.copy(window[c, t][:, cols], bank[:])
+                if t == 0:
+                    nc.vector.tensor_copy(twin[c, t, h], window[c, t][:, cols])
+                else:
+                    nc.sync.dma_start(twin[c, t, h], window[c, t][:, cols])
+
+        def difference(c, t):
+            diff[c, t] = ring.tile([P, S], F32, name="diff", bufs=6)
+            for h in range(2):
+                cols = slice(h * HALF, (h + 1) * HALF)
+                nc.vector.tensor_tensor(
+                    diff[c, t][:, cols],
+                    window[c, t][:].indirect(par_sb[:, h * 32 : (h + 1) * 32]),
+                    twin[c, t, h],
+                    ALU.subtract,
+                )
+
+        def squares(c, t):
+            square[c, t] = ring.tile([P, S], F32, name="square", bufs=3)
+            planes = square[c, t][:].rearrange("p (h d v) -> p h v d", h=2, d=D)
+            source = diff[c, t][:].rearrange("p (h v d) -> p h v d", h=2, d=D)
+            if (c, t) == ("y", PACK - 1):
+                for h in range(2):
+                    nc.scalar.activation(planes[:, h], source[:, h], ACT.Square)
+            else:
+                nc.scalar.activation(planes, source, ACT.Square)
+
+        def add_turned(target, parts):
+            for n, part in enumerate(parts):
+                nc.tensor.matmul(
+                    target,
+                    lhsT=part,
+                    rhs=ident[:],
+                    start=(n == 0),
+                    stop=(n == len(parts) - 1),
+                    is_transpose=True,
+                )
+
+        def block(ap, b):
+            return ap[:, b * P : (b + 1) * P]
+
+        def distance(t, h):
+            cols = slice(h * HALF, (h + 1) * HALF)
+            bank = psum.tile([P, HALF], F32, name="sumsq", bufs=2)
+            for b in range(D):
+                add_turned(block(bank, b), [block(square[c, t][:, cols], b) for c in "xy"])
+            dist[t, h] = keep.tile([P, HALF], F32, name="dist%d%d" % (t, h))
+            nc.scalar.activation(dist[t, h][:], bank[:], ACT.Sqrt, bias=0.05)
+
+        ref_turned = {}
+
+        def turn_ref(t, h, bank):
+            ref_turned[t, h] = bank
+            for b in range(D):
+                add_turned(block(bank, b), [ref_sb[t][:, h * HALF + b : (h + 1) * HALF : D]])
+
+        lddt = {}
+
+        def error(t):
+            signed = keep.tile([P, S], F32, name="signed" if t == 0 else "signed%d" % t)
+            lddt[t] = keep.tile([P, V + S], F32, name="lddt%d" % t)
+            err[t] = lddt[t][:, V:]
+            for h in range(2):
+                nc.vector.tensor_tensor(
+                    signed[:, h * HALF : (h + 1) * HALF],
+                    dist[t, h][:],
+                    ref_turned[t, h][:],
+                    ALU.subtract,
+                )
+            for h in range(2):
+                cols = slice(h * HALF, (h + 1) * HALF)
+                nc.vector.scalar_tensor_tensor(
+                    err[t][:, cols], signed[:, cols], -1.0, signed[:, cols], ALU.mult, ALU.max
+                )
+
+        def score(t):
+            both = [scores[:, (2 * (t % 2) + n) * S : (2 * (t % 2) + n + 1) * S] for n in range(2)]
+            width = HALF if t == PACK - 1 else S
+            for start in range(0, S, width):
+                cols = slice(start, start + width)
+                for s, bias in zip(both, (2.0, 5.0)):
+                    nc.scalar.activation(
+                        s[:, cols], err[t][:, cols], ACT.Sigmoid, bias=bias, scale=-4.0
+                    )
+            sums = psum.tile([P, V], F32, name="wide", bufs=6)
+            for h in range(2):
+                add_turned(block(sums, h), [block(s, D * h + b) for s in both for b in range(D)])
+            if t in LDDT_ON_SCALAR:
+                nc.scalar.activation(
+                    lddt[t][:, :V], sums[:], ACT.Copy, scale=eighth[:, t : t + 1]
+                )
+            else:
+                nc.vector.tensor_scalar(
+                    lddt[t][:, :V], sums[:], eighth[:, t : t + 1], None, ALU.mult
+                )
+
+        def load_wt():
+            raw = ring.tile([P, PACK, U], F32, name="big", bufs=2)
+            nc.sync.dma_start(raw[:], wt_rows)
+            return raw
+
+        hid = keep.tile([P, PACK, U], F32, name="hid")
+
+        def domains(t):
+            width = U // 2 if t == PACK - 1 else U
+            for start in range(0, U, width):
+                cols = slice(start, start + width)
+                nc.vector.tensor_tensor(
+                    hid[:, t, cols],
+                    lddt[t][:].indirect(dom_sb[:, start // LIST : (start + width) // LIST]),
+                    factor[:, t, cols],
+                    ALU.mult,
+                )
+
+        first = deal("w1a", w1_raw, 0, 1, "vector")
+        rest = deal("w1b", w1_raw, 1, PACK, "scalar")
+        codes, scales = quantise("w1a", first, P)
+        weights["x", 0] = (codes, scales, 0)
+        codes, scales = quantise("w1b", rest, 3 * P)
+        for t in range(1, PACK):
+            weights["x", t] = (codes, scales, (t - 1) * P)
+        second = deal("w2", w2_raw, 0, PACK, "vector")
+        codes, scales = quantise("w2", second, H)
+        for t in range(PACK):
+            weights["y", t] = (codes, scales, t * P)
+        units = [(c, t) for t in range(PACK) for c in "xy"]
+        for c, t in [units[0], units[2], units[1]] + units[3:]:
+            product(c, t)
+        for c, t in units:
+            difference(c, t)
+        load_ref(0)
+        load_ref(1)
+        halves = [(t, h) for t in range(PACK) for h in range(2)]
+        for t in range(PACK):
+            squares("x", t)
+            squares("y", t)
+            for h in range(2):
+                distance(t, h)
+        for t, h in halves[:6]:
+            turn_ref(t, h, psum.tile([P, HALF], F32, name="wide", bufs=6))
+        for t, h in halves[6:]:
+            turn_ref(t, h, psum.tile([P, HALF], F32, name="sumsq", bufs=2))
+        for t in range(PACK):
+            error(t)
+        factor = load_wt()
+        scores = ring.tile([P, 8 * HALF], F32, name="big", bufs=2)
+        w3_raw = keep.tile([P, PACK, N], F32, name="dist00")
+        nc.sync.dma_start(w3_raw[:], w3.rearrange("(p j) n -> p j n", j=PACK))
+
+        w3_bf = keep.tile([P, N * PACK], BF16, name="w3_bf", align_bytes=64)
+        nc.vector.tensor_copy(
+            w3_bf[:].rearrange("p (c i j) -> p c j i", i=4, j=PACK),
+            w3_raw[:].rearrange("p j (c i) -> p c j i", i=4),
+        )
+        w3_codes, w3_scales = quantise("w3", w3_bf, N)
+
+        for t in range(PACK):
+            score(t)
+            domains(t)
+
+        width = U // 2
+        result = keep.tile([P, U], F32, name="result")
+        for h in range(2):
+            cols = slice(h * width, (h + 1) * width)
+            hid_bf = keep.tile([P, width * PACK], BF16, name="hid_bf%d" % h, align_bytes=64)
+            dst = hid_bf[:].rearrange("p (c i t) -> p c t i", i=4, t=PACK)
+            src = hid[:, :, cols].rearrange("p t (c i) -> p c t i", i=4)
+            if h == 0:
+                nc.scalar.copy(dst, src)
+            else:
+                nc.vector.tensor_copy(dst, src)
+            codes, scales = quantise("hid%d" % h, hid_bf, width)
+            bank = psum.tile([P, width], F32, name="wide", bufs=6)
+            nc.tensor.matmul_mx(
+                out=bank[:],
+                lhsT=w3_codes[:].bitcast(FP8X4),
+                lhsT_scale=w3_scales[:],
+                rhs=codes[:].bitcast(FP8X4),
+                rhs_scale=scales[:],
+                start=True,
+                stop=True,
+            )
+            nc.scalar.copy(result[:, cols], bank[:])
+            nc.sync.dma_start(out[:, cols], result[:, cols])

@@ -16,9 +16,11 @@ ACT = mybir.ActivationFunctionType
 P = 128
 K, T, S, D, N, H, V, U = 512, 2048, 1024, 4, 128, 512, 256, 512
 PACK = 4
+LAST = PACK - 1
 HALF = 512
 LIST = 16
-LDDT_ON_SCALAR = (0,)
+SUMSQ_BANKS = 2
+WIDE_BANKS = 8 - SUMSQ_BANKS
 
 FLOPS = 2 * 2 * K * H * S + 2 * H * N * U
 
@@ -29,16 +31,24 @@ def tile_picked_ylddts_mean_p_kernel(
     nc = tc.nc
     with ExitStack() as ctx:
         keep = ctx.enter_context(tc.tile_pool(name="keep", bufs=1))
-        ring = ctx.enter_context(tc.tile_pool(name="ring", bufs=4))
         psum = ctx.enter_context(tc.psum_pool(name="psum", bufs=1))
+
+        def half(ap, h):
+            return ap[:, h * HALF : (h + 1) * HALF]
+
+        def block(ap, b):
+            return ap[:, b * P : (b + 1) * P]
+
+        def entries(list_tile, start, count):
+            return list_tile[:, start // LIST : (start + count) // LIST]
 
         offs_sb = keep.tile([P, S // LIST], U16, name="offs_sb")
         par_sb = keep.tile([P, S // LIST], U16, name="par_sb")
         dom_sb = keep.tile([P, U // LIST], U16, name="dom_sb")
         x_bytes = keep.tile([P, T], U8, name="x_bytes", align_bytes=64)
         x_codes = keep.tile([P, T], U32, name="x_codes", align_bytes=64)
-        w1_raw = ring.tile([P, PACK, H], F32, name="big", bufs=2)
-        w2_raw = ring.tile([P, PACK, H], F32, name="big", bufs=2)
+        w1_raw = keep.tile([P, PACK, H], F32, name="stage", bufs=2)
+        w2_raw = keep.tile([P, PACK, H], F32, name="stage", bufs=2)
         unit_sb = keep.tile([P, PACK], F32, name="unit_sb")
         ident = keep.tile([P, P], F32, name="ident")
 
@@ -57,17 +67,6 @@ def tile_picked_ylddts_mean_p_kernel(
         nc.sync.dma_start(w1_raw[:], w1.rearrange("(p j) c -> p j c", j=PACK))
         nc.sync.dma_start(w2_raw[:], w2.rearrange("(p j) c -> p j c", j=PACK))
         make_identity(nc, ident[:])
-
-        ref_rows = ref.rearrange("(p t) j -> p t j", t=PACK)
-        wt_rows = wt.rearrange("(p t) r -> p t r", t=PACK)
-        ref_sb = {}
-
-        def load_ref(pair):
-            both = ring.tile([P, 2, S], F32, name="big", bufs=2)
-            nc.sync.dma_start(both[:], ref_rows[:, 2 * pair : 2 * pair + 2, :])
-            for n in range(2):
-                ref_sb[2 * pair + n] = both[:, n, :]
-
         nc.sync.dma_start(unit_sb[:], unit.rearrange("(p t) o -> p (t o)", t=PACK))
 
         eighth = keep.tile([P, PACK], F32, name="eighth")
@@ -78,206 +77,206 @@ def tile_picked_ylddts_mean_p_kernel(
         picked_codes = []
         for h in range(2):
             codes = keep.tile([P, HALF], U32, name="picked_codes%d" % h, align_bytes=64)
-            nc.vector.tensor_copy(
-                codes[:], x_codes[:].indirect(offs_sb[:, h * 32 : (h + 1) * 32])
-            )
+            nc.vector.tensor_copy(codes[:], x_codes[:].indirect(entries(offs_sb, h * HALF, HALF)))
             picked_codes.append(codes)
+
+        def quantise(name, rounded, width):
+            codes = keep.tile([P, width], U32, name=name + "_codes", align_bytes=64)
+            scales = keep.tile([P, width], U8, name=name + "_scales", align_bytes=64)
+            nc.vector.quantize_mx(out=codes[:].bitcast(FP8X4), scales=scales[:], in_=rounded[:])
+            return codes, scales
 
         weights = {}
 
-        def deal(name, raw, t0, t1, engine):
-            width = (t1 - t0) * P
-            dealt = keep.tile([P, width * PACK], BF16, name=name + "_bf", align_bytes=64)
-            dst = dealt[:].rearrange("p (t m j) -> p m j t", j=PACK, m=P)
-            src = raw[:].rearrange("p j (m t) -> p m j t", t=PACK)[:, :, :, t0:t1]
-            if engine == "vector":
-                nc.vector.tensor_copy(dst, src)
-            else:
-                nc.scalar.copy(dst, src)
-            return dealt
+        def make_weights(c, raw, first, count, copy, buffer):
+            rounded = keep.tile([P, count * P * PACK], BF16, name=buffer, align_bytes=64)
+            copy(
+                rounded[:].rearrange("p (t m j) -> p m j t", j=PACK, m=P),
+                raw[:].rearrange("p j (m t) -> p m j t", t=PACK)[:, :, :, first : first + count],
+            )
+            codes, scales = quantise("w%s%d" % (c, first), rounded, count * P)
+            for n in range(count):
+                weights[c, first + n] = (block(codes, n), block(scales, n))
 
-        def quantise(name, dealt, width):
-            codes = keep.tile([P, width], U32, name=name + "_codes", align_bytes=64)
-            scales = keep.tile([P, width], U8, name=name + "_scales", align_bytes=64)
-            nc.vector.quantize_mx(out=codes[:].bitcast(FP8X4), scales=scales[:], in_=dealt[:])
-            return codes, scales
-
-        window, twin, diff, square, dist, err = {}, {}, {}, {}, {}, {}
+        window, twin, diff, square, dist, ref_sb, ref_turned, err, lddt = [{} for n in range(9)]
 
         def product(c, t):
-            codes, scales, col = weights[c, t]
+            codes, scales = weights[c, t]
             window[c, t] = keep.tile([P, S], F32, name="window%s%d" % (c, t))
-            tag = "signed" if (c, t) == ("y", PACK - 1) else "twin%s%d" % (c, t)
-            whole = keep.tile([P, S], F32, name=tag)
+            twin[c, t] = keep.tile([P, S], F32, name="twin%s%d" % (c, t))
             for h in range(2):
-                twin[c, t, h] = whole[:, h * HALF : (h + 1) * HALF]
-            for h in range(2):
-                cols = slice(h * HALF, (h + 1) * HALF)
-                bank = psum.tile([P, HALF], F32, name="wide", bufs=6)
+                bank = psum.tile([P, HALF], F32, name="wide", bufs=WIDE_BANKS)
                 nc.tensor.matmul_mx(
                     out=bank[:],
-                    lhsT=codes[:, col : col + P].bitcast(FP8X4),
-                    lhsT_scale=scales[:, col : col + P],
+                    lhsT=codes.bitcast(FP8X4),
+                    lhsT_scale=scales,
                     rhs=picked_codes[h][:].bitcast(FP8X4),
-                    rhs_scale=picked_bytes[:, cols],
+                    rhs_scale=half(picked_bytes, h),
                     start=True,
                     stop=True,
                 )
-                nc.scalar.copy(window[c, t][:, cols], bank[:])
-                if t == 0:
-                    nc.vector.tensor_copy(twin[c, t, h], window[c, t][:, cols])
+                nc.scalar.copy(half(window[c, t], h), bank[:])
+                if (c, t) == ("x", 0):
+                    nc.vector.tensor_copy(half(twin[c, t], h), half(window[c, t], h))
                 else:
-                    nc.sync.dma_start(twin[c, t, h], window[c, t][:, cols])
+                    nc.sync.dma_start(half(twin[c, t], h), half(window[c, t], h))
 
         def difference(c, t):
-            diff[c, t] = ring.tile([P, S], F32, name="diff", bufs=6)
+            diff[c, t] = keep.tile([P, S], F32, name="diff%s%d" % (c, t))
             for h in range(2):
-                cols = slice(h * HALF, (h + 1) * HALF)
                 nc.vector.tensor_tensor(
-                    diff[c, t][:, cols],
-                    window[c, t][:].indirect(par_sb[:, h * 32 : (h + 1) * 32]),
-                    twin[c, t, h],
+                    half(diff[c, t], h),
+                    window[c, t][:].indirect(entries(par_sb, h * HALF, HALF)),
+                    half(twin[c, t], h),
                     ALU.subtract,
                 )
 
-        def squares(c, t):
-            square[c, t] = ring.tile([P, S], F32, name="square", bufs=3)
-            planes = square[c, t][:].rearrange("p (h d v) -> p h v d", h=2, d=D)
-            source = diff[c, t][:].rearrange("p (h v d) -> p h v d", h=2, d=D)
-            if (c, t) == ("y", PACK - 1):
-                for h in range(2):
-                    nc.scalar.activation(planes[:, h], source[:, h], ACT.Square)
-            else:
-                nc.scalar.activation(planes, source, ACT.Square)
+        def square_by_member(target, source):
+            nc.scalar.activation(
+                target.rearrange("p (h d v) -> p h v d", v=P, d=D),
+                source.rearrange("p (h v d) -> p h v d", v=P, d=D),
+                ACT.Square,
+            )
 
-        def add_turned(target, parts):
-            for n, part in enumerate(parts):
+        def square_x(t):
+            whole = keep.tile([P, S], F32, name="squarex%d" % t)
+            square_by_member(whole[:], diff["x", t][:])
+            for h in range(2):
+                square["x", t, h] = half(whole, h)
+
+        def square_y(t, h):
+            part = keep.tile([P, HALF], F32, name="squarey%d" % h)
+            square_by_member(part[:], half(diff["y", t], h))
+            square["y", t, h] = part[:]
+
+        def add_turned(pairs):
+            for n, (target, source) in enumerate(pairs):
                 nc.tensor.matmul(
                     target,
-                    lhsT=part,
+                    lhsT=source,
                     rhs=ident[:],
                     start=(n == 0),
-                    stop=(n == len(parts) - 1),
+                    stop=(n == len(pairs) - 1),
                     is_transpose=True,
                 )
 
-        def block(ap, b):
-            return ap[:, b * P : (b + 1) * P]
-
         def distance(t, h):
-            cols = slice(h * HALF, (h + 1) * HALF)
-            bank = psum.tile([P, HALF], F32, name="sumsq", bufs=2)
-            for b in range(D):
-                add_turned(block(bank, b), [block(square[c, t][:, cols], b) for c in "xy"])
+            bank = psum.tile([P, HALF], F32, name="sumsq", bufs=SUMSQ_BANKS)
+            add_turned(
+                [(block(bank, d), block(square[c, t, h], d)) for c in "xy" for d in range(D)]
+            )
             dist[t, h] = keep.tile([P, HALF], F32, name="dist%d%d" % (t, h))
             nc.scalar.activation(dist[t, h][:], bank[:], ACT.Sqrt, bias=0.05)
 
-        ref_turned = {}
+        def load_ref(pair):
+            both = keep.tile([P, 2, S], F32, name="stage", bufs=2)
+            rows = ref.rearrange("(p t) j -> p t j", t=PACK)
+            nc.sync.dma_start(both[:], rows[:, 2 * pair : 2 * pair + 2, :])
+            for n in range(2):
+                ref_sb[2 * pair + n] = both[:, n, :]
 
         def turn_ref(t, h, bank):
             ref_turned[t, h] = bank
-            for b in range(D):
-                add_turned(block(bank, b), [ref_sb[t][:, h * HALF + b : (h + 1) * HALF : D]])
-
-        lddt = {}
+            for d in range(D):
+                add_turned([(block(bank, d), ref_sb[t][:, h * HALF + d : (h + 1) * HALF : D])])
 
         def error(t):
-            signed = keep.tile([P, S], F32, name="signed" if t == 0 else "signed%d" % t)
+            signed = keep.tile([P, S], F32, name="twiny%d" % LAST if t == 0 else "twinx%d" % t)
             lddt[t] = keep.tile([P, V + S], F32, name="lddt%d" % t)
             err[t] = lddt[t][:, V:]
             for h in range(2):
                 nc.vector.tensor_tensor(
-                    signed[:, h * HALF : (h + 1) * HALF],
-                    dist[t, h][:],
-                    ref_turned[t, h][:],
-                    ALU.subtract,
+                    half(signed, h), dist[t, h][:], ref_turned[t, h][:], ALU.subtract
                 )
-            for h in range(2):
-                cols = slice(h * HALF, (h + 1) * HALF)
-                nc.vector.scalar_tensor_tensor(
-                    err[t][:, cols], signed[:, cols], -1.0, signed[:, cols], ALU.mult, ALU.max
-                )
+            nc.vector.scalar_tensor_tensor(err[t], signed[:], -1.0, signed[:], ALU.mult, ALU.max)
 
         def score(t):
             both = [scores[:, (2 * (t % 2) + n) * S : (2 * (t % 2) + n + 1) * S] for n in range(2)]
-            width = HALF if t == PACK - 1 else S
-            for start in range(0, S, width):
+            pieces = [(n, h * HALF, HALF) for h in range(2) for n in range(2)]
+            if t == LAST:
+                pieces[-1:] = [(1, HALF, HALF - P), (1, S - P, P)]
+            for n, start, width in pieces:
                 cols = slice(start, start + width)
-                for s, bias in zip(both, (2.0, 5.0)):
-                    nc.scalar.activation(
-                        s[:, cols], err[t][:, cols], ACT.Sigmoid, bias=bias, scale=-4.0
-                    )
-            sums = psum.tile([P, V], F32, name="wide", bufs=6)
-            for h in range(2):
-                add_turned(block(sums, h), [block(s, D * h + b) for s in both for b in range(D)])
-            if t in LDDT_ON_SCALAR:
                 nc.scalar.activation(
-                    lddt[t][:, :V], sums[:], ACT.Copy, scale=eighth[:, t : t + 1]
+                    both[n][:, cols], err[t][:, cols], ACT.Sigmoid, bias=(2.0, 5.0)[n], scale=-4.0
                 )
-            else:
-                nc.vector.tensor_scalar(
-                    lddt[t][:, :V], sums[:], eighth[:, t : t + 1], None, ALU.mult
-                )
+            factor = eighth[:, t : t + 1]
 
-        def load_wt():
-            raw = ring.tile([P, PACK, U], F32, name="big", bufs=2)
-            nc.sync.dma_start(raw[:], wt_rows)
-            return raw
+            def add_half(target, h):
+                add_turned([(target, block(s, D * h + d)) for s in both for d in range(D)])
+
+            if t == LAST:
+                for h in range(2):
+                    sums = psum.tile([P, P], F32, name="wide", bufs=WIDE_BANKS)
+                    add_half(sums[:], h)
+                    nc.vector.tensor_scalar(block(lddt[t], h), sums[:], factor, None, ALU.mult)
+                return
+            sums = psum.tile([P, V], F32, name="wide", bufs=WIDE_BANKS)
+            for h in range(2):
+                add_half(block(sums, h), h)
+            if t == 0:
+                nc.scalar.activation(lddt[t][:, :V], sums[:], ACT.Copy, scale=factor)
+            else:
+                nc.vector.tensor_scalar(lddt[t][:, :V], sums[:], factor, None, ALU.mult)
 
         hid = keep.tile([P, PACK, U], F32, name="hid")
 
         def domains(t):
-            width = U // 2 if t == PACK - 1 else U
+            width = U // 2 if t == LAST else U
             for start in range(0, U, width):
                 cols = slice(start, start + width)
                 nc.vector.tensor_tensor(
                     hid[:, t, cols],
-                    lddt[t][:].indirect(dom_sb[:, start // LIST : (start + width) // LIST]),
-                    factor[:, t, cols],
+                    lddt[t][:].indirect(entries(dom_sb, start, width)),
+                    wt_sb[:, t, cols],
                     ALU.mult,
                 )
 
-        first = deal("w1a", w1_raw, 0, 1, "vector")
-        rest = deal("w1b", w1_raw, 1, PACK, "scalar")
-        codes, scales = quantise("w1a", first, P)
-        weights["x", 0] = (codes, scales, 0)
-        codes, scales = quantise("w1b", rest, 3 * P)
-        for t in range(1, PACK):
-            weights["x", t] = (codes, scales, (t - 1) * P)
-        second = deal("w2", w2_raw, 0, PACK, "vector")
-        codes, scales = quantise("w2", second, H)
+        def interleave(copy, rounded, rows):
+            copy(
+                rounded[:].rearrange("p (c i j) -> p c j i", i=4, j=PACK),
+                rows.rearrange("p j (c i) -> p c j i", i=4),
+            )
+
+        make_weights("x", w1_raw, 0, 1, nc.scalar.copy, "rounded_a")
+        make_weights("x", w1_raw, 1, 1, nc.scalar.copy, "rounded_b")
+        make_weights("x", w1_raw, 2, 2, nc.vector.tensor_copy, "rounded_a")
         for t in range(PACK):
-            weights["y", t] = (codes, scales, t * P)
-        units = [(c, t) for t in range(PACK) for c in "xy"]
-        for c, t in [units[0], units[2], units[1]] + units[3:]:
-            product(c, t)
-        for c, t in units:
-            difference(c, t)
-        load_ref(0)
-        load_ref(1)
+            product("x", t)
+        make_weights("y", w2_raw, 0, 2, nc.vector.tensor_copy, "rounded_c")
+        make_weights("y", w2_raw, 2, 2, nc.vector.tensor_copy, "rounded_d")
+        for t in range(PACK):
+            product("y", t)
+
+        for c in "xy":
+            for t in range(PACK):
+                difference(c, t)
+        for t in range(PACK):
+            square_x(t)
         halves = [(t, h) for t in range(PACK) for h in range(2)]
-        for t in range(PACK):
-            squares("x", t)
-            squares("y", t)
-            for h in range(2):
-                distance(t, h)
-        for t, h in halves[:6]:
-            turn_ref(t, h, psum.tile([P, HALF], F32, name="wide", bufs=6))
-        for t, h in halves[6:]:
-            turn_ref(t, h, psum.tile([P, HALF], F32, name="sumsq", bufs=2))
+        for n, (t, h) in enumerate(halves):
+            square_y(t, h)
+            if n > 0:
+                distance(*halves[n - 1])
+        distance(*halves[-1])
+
+        for pair in range(2):
+            load_ref(pair)
+        for t, h in halves[:WIDE_BANKS]:
+            turn_ref(t, h, psum.tile([P, HALF], F32, name="wide", bufs=WIDE_BANKS))
+        for t, h in halves[WIDE_BANKS:]:
+            turn_ref(t, h, psum.tile([P, HALF], F32, name="sumsq", bufs=SUMSQ_BANKS))
         for t in range(PACK):
             error(t)
-        factor = load_wt()
-        scores = ring.tile([P, 8 * HALF], F32, name="big", bufs=2)
-        w3_raw = keep.tile([P, PACK, N], F32, name="dist00")
-        nc.sync.dma_start(w3_raw[:], w3.rearrange("(p j) n -> p j n", j=PACK))
 
-        w3_bf = keep.tile([P, N * PACK], BF16, name="w3_bf", align_bytes=64)
-        nc.vector.tensor_copy(
-            w3_bf[:].rearrange("p (c i j) -> p c j i", i=4, j=PACK),
-            w3_raw[:].rearrange("p j (c i) -> p c j i", i=4),
-        )
-        w3_codes, w3_scales = quantise("w3", w3_bf, N)
+        wt_sb = keep.tile([P, PACK, U], F32, name="diffx1")
+        nc.sync.dma_start(wt_sb[:], wt.rearrange("(p t) r -> p t r", t=PACK))
+        scores = keep.tile([P, 2 * 2 * S], F32, name="squarey1")
+        w3_raw = keep.tile([P, PACK, N], F32, name="twinx0")
+        nc.sync.dma_start(w3_raw[:], w3.rearrange("(p j) n -> p j n", j=PACK))
+        w3_rounded = keep.tile([P, N * PACK], BF16, name="w3_rounded", align_bytes=64)
+        interleave(nc.scalar.copy, w3_rounded, w3_raw[:])
+        w3_codes, w3_scales = quantise("w3", w3_rounded, N)
 
         for t in range(PACK):
             score(t)
@@ -285,17 +284,12 @@ def tile_picked_ylddts_mean_p_kernel(
 
         width = U // 2
         result = keep.tile([P, U], F32, name="result")
-        for h in range(2):
+        for h, copy in enumerate((nc.scalar.copy, nc.vector.tensor_copy)):
             cols = slice(h * width, (h + 1) * width)
-            hid_bf = keep.tile([P, width * PACK], BF16, name="hid_bf%d" % h, align_bytes=64)
-            dst = hid_bf[:].rearrange("p (c i t) -> p c t i", i=4, t=PACK)
-            src = hid[:, :, cols].rearrange("p t (c i) -> p c t i", i=4)
-            if h == 0:
-                nc.scalar.copy(dst, src)
-            else:
-                nc.vector.tensor_copy(dst, src)
-            codes, scales = quantise("hid%d" % h, hid_bf, width)
-            bank = psum.tile([P, width], F32, name="wide", bufs=6)
+            rounded = keep.tile([P, width * PACK], BF16, name="hid_rounded%d" % h, align_bytes=64)
+            interleave(copy, rounded, hid[:, :, cols])
+            codes, scales = quantise("hid%d" % h, rounded, width)
+            bank = psum.tile([P, width], F32, name="wide", bufs=WIDE_BANKS)
             nc.tensor.matmul_mx(
                 out=bank[:],
                 lhsT=w3_codes[:].bitcast(FP8X4),

@@ -238,6 +238,9 @@ def tile_picked_ylddts_mean_p_kernel(
                 rows.rearrange("p j (c i) -> p c j i", i=4),
             )
 
+        warm = keep.tile([P, 1], F32, name="warm")
+        nc.scalar.activation(warm[:], ident[:, 0:1], ACT.Sqrt)
+
         make_weights("x", w1_raw, 0, 1, nc.scalar.copy, "rounded_a")
         make_weights("x", w1_raw, 1, 1, nc.scalar.copy, "rounded_b")
         make_weights("x", w1_raw, 2, 2, nc.vector.tensor_copy, "rounded_a")

@@ -47,8 +47,8 @@ def tile_picked_ylddts_mean_p_kernel(
         dom_sb = keep.tile([P, U // LIST], U16, name="dom_sb")
         x_bytes = keep.tile([P, T], U8, name="x_bytes", align_bytes=64)
         x_codes = keep.tile([P, T], U32, name="x_codes", align_bytes=64)
-        w1_raw = keep.tile([P, PACK, H], F32, name="stage", bufs=2)
-        w2_raw = keep.tile([P, PACK, H], F32, name="stage", bufs=2)
+        w1_raw = keep.tile([P, PACK, H], F32, name="w1_raw")
+        w2_raw = keep.tile([P, PACK, H], F32, name="w2_raw")
         unit_sb = keep.tile([P, PACK], F32, name="unit_sb")
         ident = keep.tile([P, P], F32, name="ident")
 
@@ -88,13 +88,17 @@ def tile_picked_ylddts_mean_p_kernel(
 
         weights = {}
 
-        def make_weights(c, raw, first, count, copy, buffer):
-            rounded = keep.tile([P, count * P * PACK], BF16, name=buffer, align_bytes=64)
-            copy(
-                rounded[:].rearrange("p (t m j) -> p m j t", j=PACK, m=P),
-                raw[:].rearrange("p j (m t) -> p m j t", t=PACK)[:, :, :, first : first + count],
-            )
-            codes, scales = quantise("w%s%d" % (c, first), rounded, count * P)
+        def round_weights(c, raw, shares):
+            rounded = keep.tile([P, H * PACK], BF16, name="rounded" + c, align_bytes=64)
+            target = rounded[:].rearrange("p (t m j) -> p m j t", j=PACK, m=P)
+            source = raw[:].rearrange("p j (m t) -> p m j t", t=PACK)
+            for copy, part in shares:
+                copy(target[:, part], source[:, part])
+            return rounded
+
+        def make_weights(c, rounded, first, count):
+            columns = rounded[:, first * P * PACK : (first + count) * P * PACK]
+            codes, scales = quantise("w%s%d" % (c, first), columns, count * P)
             for n in range(count):
                 weights[c, first + n] = (block(codes, n), block(scales, n))
 
@@ -168,12 +172,9 @@ def tile_picked_ylddts_mean_p_kernel(
             dist[t, h] = keep.tile([P, HALF], F32, name="dist%d%d" % (t, h))
             nc.scalar.activation(dist[t, h][:], bank[:], ACT.Sqrt, bias=0.05)
 
-        def load_ref(pair):
-            both = keep.tile([P, 2, S], F32, name="stage", bufs=2)
-            rows = ref.rearrange("(p t) j -> p t j", t=PACK)
-            nc.sync.dma_start(both[:], rows[:, 2 * pair : 2 * pair + 2, :])
-            for n in range(2):
-                ref_sb[2 * pair + n] = both[:, n, :]
+        def load_ref(t):
+            ref_sb[t] = keep.tile([P, S], F32, name="windowx%d" % t if t > 0 else "w1_raw")
+            nc.sync.dma_start(ref_sb[t][:], ref.rearrange("(p t) j -> p t j", t=PACK)[:, t, :])
 
         def turn_ref(t, h, bank):
             ref_turned[t, h] = bank
@@ -232,22 +233,27 @@ def tile_picked_ylddts_mean_p_kernel(
                     ALU.mult,
                 )
 
-        def interleave(copy, rounded, rows):
+        def interleave(copy, rounded, rows, first=0, count=PACK):
+            places = slice(first, first + count)
             copy(
-                rounded[:].rearrange("p (c i j) -> p c j i", i=4, j=PACK),
-                rows.rearrange("p j (c i) -> p c j i", i=4),
+                rounded[:].rearrange("p (c i j) -> p c j i", i=4, j=PACK)[:, :, places, :],
+                rows.rearrange("p j (c i) -> p c j i", i=4)[:, :, places, :],
             )
 
         warm = keep.tile([P, 1], F32, name="warm")
         nc.scalar.activation(warm[:], ident[:, 0:1], ACT.Sqrt)
 
-        make_weights("x", w1_raw, 0, 1, nc.scalar.copy, "rounded_a")
-        make_weights("x", w1_raw, 1, 1, nc.scalar.copy, "rounded_b")
-        make_weights("x", w1_raw, 2, 2, nc.vector.tensor_copy, "rounded_a")
+        w1_rounded = round_weights(
+            "x",
+            w1_raw,
+            [(nc.scalar.copy, slice(0, P // 2)), (nc.vector.tensor_copy, slice(P // 2, P))],
+        )
+        make_weights("x", w1_rounded, 0, 1)
+        make_weights("x", w1_rounded, 1, PACK - 1)
         for t in range(PACK):
             product("x", t)
-        make_weights("y", w2_raw, 0, 2, nc.vector.tensor_copy, "rounded_c")
-        make_weights("y", w2_raw, 2, 2, nc.vector.tensor_copy, "rounded_d")
+        w2_rounded = round_weights("y", w2_raw, [(nc.vector.tensor_copy, slice(0, P))])
+        make_weights("y", w2_rounded, 0, PACK)
         for t in range(PACK):
             product("y", t)
 
@@ -263,8 +269,8 @@ def tile_picked_ylddts_mean_p_kernel(
                 distance(*halves[n - 1])
         distance(*halves[-1])
 
-        for pair in range(2):
-            load_ref(pair)
+        for t in range(PACK):
+            load_ref(t)
         for t, h in halves[:WIDE_BANKS]:
             turn_ref(t, h, psum.tile([P, HALF], F32, name="wide", bufs=WIDE_BANKS))
         for t, h in halves[WIDE_BANKS:]:
@@ -275,7 +281,7 @@ def tile_picked_ylddts_mean_p_kernel(
         wt_sb = keep.tile([P, PACK, U], F32, name="diffx1")
         nc.sync.dma_start(wt_sb[:], wt.rearrange("(p t) r -> p t r", t=PACK))
         scores = keep.tile([P, 2 * 2 * S], F32, name="squarey1")
-        w3_raw = keep.tile([P, PACK, N], F32, name="twinx0")
+        w3_raw = keep.tile([P, PACK, N], F32, name="diffx2")
         nc.sync.dma_start(w3_raw[:], w3.rearrange("(p j) n -> p j n", j=PACK))
         w3_rounded = keep.tile([P, N * PACK], BF16, name="w3_rounded", align_bytes=64)
         interleave(nc.scalar.copy, w3_rounded, w3_raw[:])
@@ -287,11 +293,15 @@ def tile_picked_ylddts_mean_p_kernel(
 
         width = U // 2
         result = keep.tile([P, U], F32, name="result")
+        hid_rounded = []
+        for h in range(2):
+            rounded = keep.tile([P, width * PACK], BF16, name="hid_rounded%d" % h, align_bytes=64)
+            interleave(nc.scalar.copy, rounded, hid[:, :, h * width : (h + 1) * width], 0, 2)
+            hid_rounded.append(rounded)
         for h, copy in enumerate((nc.scalar.copy, nc.vector.tensor_copy)):
             cols = slice(h * width, (h + 1) * width)
-            rounded = keep.tile([P, width * PACK], BF16, name="hid_rounded%d" % h, align_bytes=64)
-            interleave(copy, rounded, hid[:, :, cols])
-            codes, scales = quantise("hid%d" % h, rounded, width)
+            interleave(copy, hid_rounded[h], hid[:, :, cols], 2, 2)
+            codes, scales = quantise("hid%d" % h, hid_rounded[h], width)
             bank = psum.tile([P, width], F32, name="wide", bufs=WIDE_BANKS)
             nc.tensor.matmul_mx(
                 out=bank[:],

from contextlib import ExitStack

import concourse.mybir as mybir
from concourse.masks import make_identity

F32 = mybir.dt.float32
BF16 = mybir.dt.bfloat16
I32 = mybir.dt.int32
U32 = mybir.dt.uint32
U16 = mybir.dt.uint16
U8 = mybir.dt.uint8
FP8X4 = mybir.dt.float8_e4m3fn_x4
ALU = mybir.AluOpType
ACT = mybir.ActivationFunctionType

P = 128
K, T, S, D, N, H, V, U = 512, 2048, 1024, 4, 128, 512, 256, 512
PACK = 4
LAST = PACK - 1
HALF = 512
LIST = 16
SUMSQ_BANKS = 2
WIDE_BANKS = 8 - SUMSQ_BANKS

FLOPS = 2 * 2 * K * H * S + 2 * H * N * U


def tile_picked_ylddts_mean_p_kernel(
    tc, x_words, x_scales, w1, w2, ref, wt, unit, w3, offs, par, dom, out
):
    nc = tc.nc
    with ExitStack() as ctx:
        keep = ctx.enter_context(tc.tile_pool(name="keep", bufs=1))
        psum = ctx.enter_context(tc.psum_pool(name="psum", bufs=1))

        def half(ap, h):
            return ap[:, h * HALF : (h + 1) * HALF]

        def block(ap, b):
            return ap[:, b * P : (b + 1) * P]

        def entries(list_tile, start, count):
            return list_tile[:, start // LIST : (start + count) // LIST]

        offs_sb = keep.tile([P, S // LIST], U16, name="offs_sb")
        par_sb = keep.tile([P, S // LIST], U16, name="par_sb")
        dom_sb = keep.tile([P, U // LIST], U16, name="dom_sb")
        x_bytes = keep.tile([P, T], U8, name="x_bytes", align_bytes=64)
        x_codes = keep.tile([P, T], U32, name="x_codes", align_bytes=64)
        w1_raw = keep.tile([P, PACK, H], F32, name="w1_raw")
        w2_raw = keep.tile([P, PACK, H], F32, name="w2_raw")
        unit_sb = keep.tile([P, PACK], F32, name="unit_sb")
        ident = keep.tile([P, P], F32, name="ident")

        nc.gpsimd.memset(x_bytes[:].bitcast(I32), 0)
        nc.sync.dma_start(offs_sb[:], offs)
        nc.sync.dma_start(par_sb[:], par)
        nc.sync.dma_start(dom_sb[:], dom)
        for q in range(4):
            nc.sync.dma_start(
                x_bytes[32 * q : 32 * q + 4, :].bitcast(I32),
                x_scales[0, 4 * q : 4 * q + 4, :].bitcast(I32),
            )
        nc.sync.dma_start(
            x_codes[:].bitcast(I32), x_words[0].rearrange("p n t -> p (n t)").bitcast(I32)
        )
        nc.sync.dma_start(w1_raw[:], w1.rearrange("(p j) c -> p j c", j=PACK))
        nc.sync.dma_start(w2_raw[:], w2.rearrange("(p j) c -> p j c", j=PACK))
        make_identity(nc, ident[:])
        nc.sync.dma_start(unit_sb[:], unit.rearrange("(p t) o -> p (t o)", t=PACK))

        eighth = keep.tile([P, PACK], F32, name="eighth")
        nc.gpsimd.tensor_scalar(eighth[:], unit_sb[:], 0.125, 0.0, ALU.mult, ALU.add)

        picked_bytes = keep.tile([P, S], U8, name="picked_bytes", align_bytes=64)
        nc.vector.tensor_copy(picked_bytes[:], x_bytes[:].indirect(offs_sb[:]))
        picked_codes = []
        for h in range(2):
            codes = keep.tile([P, HALF], U32, name="picked_codes%d" % h, align_bytes=64)
            nc.vector.tensor_copy(codes[:], x_codes[:].indirect(entries(offs_sb, h * HALF, HALF)))
            picked_codes.append(codes)

        def quantise(name, rounded, width):
            codes = keep.tile([P, width], U32, name=name + "_codes", align_bytes=64)
            scales = keep.tile([P, width], U8, name=name + "_scales", align_bytes=64)
            nc.vector.quantize_mx(out=codes[:].bitcast(FP8X4), scales=scales[:], in_=rounded[:])
            return codes, scales

        weights = {}

        def round_weights(c, raw, shares):
            rounded = keep.tile([P, H * PACK], BF16, name="rounded" + c, align_bytes=64)
            target = rounded[:].rearrange("p (t m j) -> p m j t", j=PACK, m=P)
            source = raw[:].rearrange("p j (m t) -> p m j t", t=PACK)
            for copy, part in shares:
                copy(target[:, part], source[:, part])
            return rounded

        def make_weights(c, rounded, first, count):
            columns = rounded[:, first * P * PACK : (first + count) * P * PACK]
            codes, scales = quantise("w%s%d" % (c, first), columns, count * P)
            for n in range(count):
                weights[c, first + n] = (block(codes, n), block(scales, n))

        window, twin, diff, square, dist, ref_sb, ref_turned, err, lddt = [{} for n in range(9)]

        def product(c, t):
            codes, scales = weights[c, t]
            window[c, t] = keep.tile([P, S], F32, name="window%s%d" % (c, t))
            twin[c, t] = keep.tile([P, S], F32, name="twin%s%d" % (c, t))
            for h in range(2):
                bank = psum.tile([P, HALF], F32, name="wide", bufs=WIDE_BANKS)
                nc.tensor.matmul_mx(
                    out=bank[:],
                    lhsT=codes.bitcast(FP8X4),
                    lhsT_scale=scales,
                    rhs=picked_codes[h][:].bitcast(FP8X4),
                    rhs_scale=half(picked_bytes, h),
                    start=True,
                    stop=True,
                )
                nc.scalar.copy(half(window[c, t], h), bank[:])
                if (c, t) == ("x", 0):
                    nc.vector.tensor_copy(half(twin[c, t], h), half(window[c, t], h))
                else:
                    nc.sync.dma_start(half(twin[c, t], h), half(window[c, t], h))

        def difference(c, t):
            diff[c, t] = keep.tile([P, S], F32, name="diff%s%d" % (c, t))
            for h in range(2):
                nc.vector.tensor_tensor(
                    half(diff[c, t], h),
                    window[c, t][:].indirect(entries(par_sb, h * HALF, HALF)),
                    half(twin[c, t], h),
                    ALU.subtract,
                )

        def square_by_member(target, source):
            nc.scalar.activation(
                target.rearrange("p (h d v) -> p h v d", v=P, d=D),
                source.rearrange("p (h v d) -> p h v d", v=P, d=D),
                ACT.Square,
            )

        def square_x(t):
            whole = keep.tile([P, S], F32, name="squarex%d" % t)
            square_by_member(whole[:], diff["x", t][:])
            for h in range(2):
                square["x", t, h] = half(whole, h)

        def square_y(t, h):
            part = keep.tile([P, HALF], F32, name="squarey%d" % h)
            square_by_member(part[:], half(diff["y", t], h))
            square["y", t, h] = part[:]

        def add_turned(pairs):
            for n, (target, source) in enumerate(pairs):
                nc.tensor.matmul(
                    target,
                    lhsT=source,
                    rhs=ident[:],
                    start=(n == 0),
                    stop=(n == len(pairs) - 1),
                    is_transpose=True,
                )

        def distance(t, h):
            bank = psum.tile([P, HALF], F32, name="sumsq", bufs=SUMSQ_BANKS)
            add_turned(
                [(block(bank, d), block(square[c, t, h], d)) for c in "xy" for d in range(D)]
            )
            dist[t, h] = keep.tile([P, HALF], F32, name="dist%d%d" % (t, h))
            nc.scalar.activation(dist[t, h][:], bank[:], ACT.Sqrt, bias=0.05)

        def load_ref(t):
            ref_sb[t] = keep.tile([P, S], F32, name="windowx%d" % t if t > 0 else "w1_raw")
            nc.sync.dma_start(ref_sb[t][:], ref.rearrange("(p t) j -> p t j", t=PACK)[:, t, :])

        def turn_ref(t, h, bank):
            ref_turned[t, h] = bank
            for d in range(D):
                add_turned([(block(bank, d), ref_sb[t][:, h * HALF + d : (h + 1) * HALF : D])])

        def error(t):
            signed = keep.tile([P, S], F32, name="twiny%d" % LAST if t == 0 else "twinx%d" % t)
            lddt[t] = keep.tile([P, V + S], F32, name="lddt%d" % t)
            err[t] = lddt[t][:, V:]
            for h in range(2):
                nc.vector.tensor_tensor(
                    half(signed, h), dist[t, h][:], ref_turned[t, h][:], ALU.subtract
                )
            nc.vector.scalar_tensor_tensor(err[t], signed[:], -1.0, signed[:], ALU.mult, ALU.max)

        def score(t):
            both = [scores[:, (2 * (t % 2) + n) * S : (2 * (t % 2) + n + 1) * S] for n in range(2)]
            pieces = [(n, h * HALF, HALF) for h in range(2) for n in range(2)]
            if t == LAST:
                pieces[-1:] = [(1, HALF, HALF - P), (1, S - P, P)]
            for n, start, width in pieces:
                cols = slice(start, start + width)
                nc.scalar.activation(
                    both[n][:, cols], err[t][:, cols], ACT.Sigmoid, bias=(2.0, 5.0)[n], scale=-4.0
                )
            factor = eighth[:, t : t + 1]

            def add_half(target, h):
                add_turned([(target, block(s, D * h + d)) for s in both for d in range(D)])

            if t == LAST:
                for h in range(2):
                    sums = psum.tile([P, P], F32, name="wide", bufs=WIDE_BANKS)
                    add_half(sums[:], h)
                    nc.vector.tensor_scalar(block(lddt[t], h), sums[:], factor, None, ALU.mult)
                return
            sums = psum.tile([P, V], F32, name="wide", bufs=WIDE_BANKS)
            for h in range(2):
                add_half(block(sums, h), h)
            if t == 0:
                nc.scalar.activation(lddt[t][:, :V], sums[:], ACT.Copy, scale=factor)
            else:
                nc.vector.tensor_scalar(lddt[t][:, :V], sums[:], factor, None, ALU.mult)

        hid = keep.tile([P, PACK, U], F32, name="hid")

        def domains(t):
            width = U // 2 if t == LAST else U
            for start in range(0, U, width):
                cols = slice(start, start + width)
                nc.vector.tensor_tensor(
                    hid[:, t, cols],
                    lddt[t][:].indirect(entries(dom_sb, start, width)),
                    wt_sb[:, t, cols],
                    ALU.mult,
                )

        def interleave(copy, rounded, rows, first=0, count=PACK):
            places = slice(first, first + count)
            copy(
                rounded[:].rearrange("p (c i j) -> p c j i", i=4, j=PACK)[:, :, places, :],
                rows.rearrange("p j (c i) -> p c j i", i=4)[:, :, places, :],
            )

        warm = keep.tile([P, 1], F32, name="warm")
        nc.scalar.activation(warm[:], ident[:, 0:1], ACT.Sqrt)

        w1_rounded = round_weights(
            "x",
            w1_raw,
            [(nc.scalar.copy, slice(0, P // 2)), (nc.vector.tensor_copy, slice(P // 2, P))],
        )
        make_weights("x", w1_rounded, 0, 1)
        make_weights("x", w1_rounded, 1, PACK - 1)
        for t in range(PACK):
            product("x", t)
        w2_rounded = round_weights("y", w2_raw, [(nc.vector.tensor_copy, slice(0, P))])
        make_weights("y", w2_rounded, 0, PACK)
        for t in range(PACK):
            product("y", t)

        for c in "xy":
            for t in range(PACK):
                difference(c, t)
        for t in range(PACK):
            square_x(t)
        halves = [(t, h) for t in range(PACK) for h in range(2)]
        for n, (t, h) in enumerate(halves):
            square_y(t, h)
            if n > 0:
                distance(*halves[n - 1])
        distance(*halves[-1])

        for t in range(PACK):
            load_ref(t)
        for t, h in halves[:WIDE_BANKS]:
            turn_ref(t, h, psum.tile([P, HALF], F32, name="wide", bufs=WIDE_BANKS))
        for t, h in halves[WIDE_BANKS:]:
            turn_ref(t, h, psum.tile([P, HALF], F32, name="sumsq", bufs=SUMSQ_BANKS))
        for t in range(PACK):
            error(t)

        wt_sb = keep.tile([P, PACK, U], F32, name="diffx1")
        nc.sync.dma_start(wt_sb[:], wt.rearrange("(p t) r -> p t r", t=PACK))
        scores = keep.tile([P, 2 * 2 * S], F32, name="squarey1")
        w3_raw = keep.tile([P, PACK, N], F32, name="diffx2")
        nc.sync.dma_start(w3_raw[:], w3.rearrange("(p j) n -> p j n", j=PACK))
        w3_rounded = keep.tile([P, N * PACK], BF16, name="w3_rounded", align_bytes=64)
        interleave(nc.scalar.copy, w3_rounded, w3_raw[:])
        w3_codes, w3_scales = quantise("w3", w3_rounded, N)

        for t in range(PACK):
            score(t)
            domains(t)

        width = U // 2
        result = keep.tile([P, U], F32, name="result")
        hid_rounded = []
        for h in range(2):
            rounded = keep.tile([P, width * PACK], BF16, name="hid_rounded%d" % h, align_bytes=64)
            interleave(nc.scalar.copy, rounded, hid[:, :, h * width : (h + 1) * width], 0, 2)
            hid_rounded.append(rounded)
        for h, copy in enumerate((nc.scalar.copy, nc.vector.tensor_copy)):
            cols = slice(h * width, (h + 1) * width)
            interleave(copy, hid_rounded[h], hid[:, :, cols], 2, 2)
            codes, scales = quantise("hid%d" % h, hid_rounded[h], width)
            bank = psum.tile([P, width], F32, name="wide", bufs=WIDE_BANKS)
            nc.tensor.matmul_mx(
                out=bank[:],
                lhsT=w3_codes[:].bitcast(FP8X4),
                lhsT_scale=w3_scales[:],
                rhs=codes[:].bitcast(FP8X4),
                rhs_scale=scales[:],
                start=True,
                stop=True,
            )
            nc.scalar.copy(result[:, cols], bank[:])
            nc.sync.dma_start(out[:, cols], result[:, cols])
